import numpy as np
CORES = [0,4,1,5,2,6,3,7]
N = 8
ROOT = 4
def setup_inputs(rng):
    return {"x": rng.standard_normal((N, 128, N * 2), dtype=np.float32)}
def reference(x):
    return {"y": np.stack([x[ROOT][:, r * 2:(r + 1) * 2] for r in range(N)])}

from concourse.bass import DstId, RemoteDMATransfer

BLOCK = 2
ENGINES = 2

SCRATCH = {
    "stage": ("sbuf", [128, 16], "float32"),
    "land": ("sbuf", [128, BLOCK], "float32"),
}
SEMAPHORES = ["loaded", "read", "arrived", "stored"]


def rank_program(g, core, T, topo):
    rank = T.rank_of(core)
    if rank is None:
        return
    root = T.root

    if rank != root:
        g.wait_ge(T.sem.arrived, ENGINES)
        g.dma_start(T.y[:, :], T.land[:, :]).then_inc(T.sem.stored, 16)
        g.wait_ge(T.sem.stored, 16)
        return

    g.dma_start(T.stage[:, :], T.x[:, :]).then_inc(T.sem.loaded, 16)
    g.dma_start(T.y[:, :], T.x[:, root * BLOCK:(root + 1) * BLOCK]).then_inc(T.sem.stored, 16)
    g.wait_ge(T.sem.loaded, 16)

    transfers = []
    for k, r in enumerate(r for r in range(len(T.cores)) if r != root):
        dst = T.cores[r]
        rid, pid, sengine = topo.addr(dst)
        transfers.append(RemoteDMATransfer(
            dst_ids=[DstId(rid=rid, pnc=pid)],
            dma_engine_mask=((1 << ENGINES) - 1) << (k * ENGINES),
            remote_sem=T.sem.arrived,
            src=T.stage[:, r * BLOCK:(r + 1) * BLOCK],
            dst=T.land[:, :],
        ))
    g.remote_dma_fused(transfers, local_sem=T.sem.read)

    g.wait_ge(T.sem.read, ENGINES * len(transfers))
    g.wait_ge(T.sem.stored, 16)
